import numpy as np
import ml_dtypes


def mxq(x, axis, fmt="e4m3"):
    dtype, down = {"e4m3": (ml_dtypes.float8_e4m3fn, 7), "e5m2": (ml_dtypes.float8_e5m2, 14)}[fmt]
    v = np.moveaxis(np.asarray(x, np.float32).astype(ml_dtypes.bfloat16).astype(np.float64), axis, -1)
    blocks = v.reshape(v.shape[:-1] + (-1, 32))
    amax = np.abs(blocks).max(-1, keepdims=True)
    byte = np.maximum(np.where(amax > 0, np.frexp(amax)[1] - 1 + 127, 0) - down, 1)
    scale = np.exp2(byte - 127.0)
    codes = (blocks / scale).astype(np.float32).astype(dtype).astype(np.float64)
    return np.moveaxis((codes * scale).reshape(v.shape), -1, axis)


WIDE = False


def mx_kscale(k):
    if not WIDE:
        return np.ones(k)
    levels = np.array([10, -10, 5, -5, 0])
    if k % 512:
        return np.exp2(np.random.permutation(np.resize(levels, k // 32))).repeat(32)
    a = np.empty((k // 512, 16))
    for p in range(k // 512):
        a[p, :8] = np.random.permutation(np.resize(levels, 8))
        for g in range(8):
            far = levels[np.abs(levels - a[p, g]) >= 10]
            a[p, g + 8] = far[np.random.randint(len(far))]
    return np.exp2(a.ravel()).repeat(32)


def f64(x):
    return np.asarray(x).astype(np.float64)


def striped(idx):
    return np.tile(idx.reshape(-1, 16).T, (8, 1)).astype(np.uint16)


def unstriped(offs):
    return offs[:16].T.reshape(-1).astype(np.int64)


def striped8(idx):
    return np.concatenate([x.reshape(-1, 16).T for x in idx]).astype(np.uint16)


def runs(offs, k):
    lists = np.stack([offs[16 * r : 16 * r + 16].T.reshape(-1) for r in range(8)]).astype(np.int64)
    return lists[np.arange(k) % 512 // 64]


def pack_weight(w):
    k, n = w.shape
    w = f64(np.asarray(w, np.float32).astype(ml_dtypes.bfloat16)).reshape(k // 32, 32, n)
    amax = np.abs(w).max(1)
    byte = np.clip(np.where(amax > 0, np.frexp(amax)[1] - 1 + 127 - 7, 1), 1, 254)
    scaled = (w * np.exp2(127.0 - byte)[:, None, :]).reshape(k, n).astype(np.float32)
    words = np.ascontiguousarray(scaled.reshape(k // 512, 128, 4, n).transpose(0, 1, 3, 2)).astype(ml_dtypes.float8_e4m3fn).view(np.uint8)
    return words, np.ascontiguousarray(byte.astype(np.uint8).reshape(k // 512, 16, n))


def unpack_weight(words, scales):
    g, p, n, _ = words.shape
    vals = np.ascontiguousarray(words).view(ml_dtypes.float8_e4m3fn).astype(np.float64) * np.repeat(np.exp2(scales.astype(np.float64) - 127.0), 8, axis=1)[..., None]
    return vals.transpose(0, 1, 3, 2).reshape(g * 512, n)


def sigmoid(v):
    return 1.0 / (1.0 + np.exp(-np.maximum(v, -700.0)))


K, T, S, V, H, W, U = 512, 2048, 512, 256, 512, 1024, 1024


def setup_inputs():
    n = np.random.standard_normal
    s = mx_kscale(K)[:, None]
    u = mx_kscale(S)
    packed_xT = pack_weight(n((K, T)) * s)
    return {
        "x_words": packed_xT[0],
        "x_scales": packed_xT[1],
        "w1": (n((K, H)) / np.sqrt(K) / s).astype(np.float32),
        "w2": (n((K, H)) / np.sqrt(K) / s).astype(np.float32),
        "ga": (np.random.uniform(0.5, 1.5, (H, 1)) * u[:, None]).astype(np.float32),
        "gb": (np.random.uniform(0.5, 1.5, (H, 1)) / u[:, None]).astype(np.float32),
        "mem": n((S, U)).astype(np.float32),
        "offs": striped(np.random.permutation(T)[:S]),
        "two": striped(np.random.permutation(T)[:V]),
        "n1": striped(np.random.randint(0, S, W)),
        "n2": striped8(np.stack([np.random.permutation(V) for _ in range(8)])),
        "n3": striped8(np.stack([np.random.permutation(V) for _ in range(8)])),
        "n4": striped(np.random.permutation(U)[:V]),
    }


def reference(x_words, x_scales, w1, w2, ga, gb, mem, offs, two, n1, n2, n3, n4):
    xq = unpack_weight(x_words, x_scales)[:, unstriped(offs)]
    a = mxq(f64(w1), 0, "e4m3").T @ xq
    mb = a[:, unstriped(n1)]
    mn = mb.reshape(H, S, 2).min(axis=2)
    mx = mb.reshape(H, S, 2).max(axis=2)
    z = f64(ga) * ((a - mn) * sigmoid(mx))
    x_two = unpack_weight(x_words, x_scales)[:, unstriped(two)]
    b = mxq(f64(w2), 0, "e4m3").T @ x_two
    pa = b[np.arange(H)[:, None], runs(n2, H)]
    pb = b[np.arange(H)[:, None], runs(n3, H)]
    z2 = f64(gb) * (np.maximum(np.maximum(b, pa), pb) - (0.5 * (np.minimum(np.minimum(b, pa), pb))))
    s = 0.0625 * ((mxq(z, 0, "e4m3").T @ mxq(z2, 0, "e4m3")))
    out = f64(mem).copy()
    out[:, unstriped(n4)] = s
    return out

@@ -1,0 +1,191 @@
+from contextlib import ExitStack
+
+import concourse.mybir as mybir
+
+K, T, S, V, H, U = 512, 2048, 512, 256, 512, 1024
+FLOPS = 2 * K * H * S + 2 * K * H * V + 2 * H * S * V
+
+F32 = mybir.dt.float32
+BF16 = mybir.dt.bfloat16
+I32 = mybir.dt.int32
+U32 = mybir.dt.uint32
+U16 = mybir.dt.uint16
+U8 = mybir.dt.uint8
+FP8X4 = mybir.dt.float8_e4m3fn_x4
+ALU = mybir.AluOpType
+ACT = mybir.ActivationFunctionType
+
+P = 128
+PACK = 4
+LINE = 4
+CHUNKS = S // P
+
+
+def tile_picked_kqghardrangepage_none_p_kernel(tc, x_words, x_scales, w1, w2, ga, gb, mem, offs, two, n1, n2, n3, n4, out):
+    nc = tc.nc
+    with ExitStack() as ctx:
+        keep = ctx.enter_context(tc.tile_pool(name="keep", bufs=1))
+        psum = ctx.enter_context(tc.psum_pool(name="psum", bufs=1))
+
+        def load_list(src, name):
+            tile = keep.tile(list(src.shape), U16, name=name)
+            nc.sync.dma_start(tile[:], src)
+            return tile
+
+        def load_gain(src, name):
+            tile = keep.tile([P, PACK], F32, name=name)
+            nc.sync.dma_start(tile[:], src.rearrange("(p t) o -> p (t o)", t=PACK))
+            return tile
+
+        def load_weight(src, cols, name):
+            tile = keep.tile([P, PACK, cols.stop - cols.start], F32, name=name)
+            nc.sync.dma_start(tile[:], src[:, cols].rearrange("(p j) c -> p j c", j=PACK))
+            return tile
+
+        def quantize(rounded, width, name):
+            codes = keep.tile([P, width], U32, name=name + "_codes", align_bytes=64)
+            scales = keep.tile([P, width], U8, name=name + "_scales", align_bytes=64)
+            nc.vector.quantize_mx(out=codes[:].bitcast(FP8X4), scales=scales[:], in_=rounded)
+            return codes, scales
+
+        def quantize_weight(parts, name):
+            dealt = keep.tile([P, PACK, P, PACK], BF16, name=name + "_dealt", align_bytes=64)
+            share = P // len(parts)
+            for i, part in enumerate(parts):
+                nc.vector.tensor_copy(
+                    out=dealt[:, :, i * share : (i + 1) * share, :].rearrange("p t m j -> p m j t"),
+                    in_=part[:].rearrange("p j (m t) -> p m j t", t=PACK),
+                )
+            return quantize(dealt[:].rearrange("p t m j -> p (t m j)"), H, name)
+
+        def product(acc, left, left_cols, right):
+            nc.tensor.matmul_mx(
+                out=acc,
+                lhsT=left[0][:, left_cols].bitcast(FP8X4),
+                lhsT_scale=left[1][:, left_cols],
+                rhs=right[0][:].bitcast(FP8X4),
+                rhs_scale=right[1][:],
+                start=True,
+                stop=True,
+            )
+
+        table_scales = keep.tile([P, T], U8, name="table_scales")
+        nc.vector.memset(table_scales[:].bitcast(I32), 0)
+        two_list = load_list(two, "two_list")
+        offs_list = load_list(offs, "offs_list")
+        w2_parts = [load_weight(w2, slice(0, H), "w2_raw")]
+        table_words = keep.tile([P, T], I32, name="table_words")
+        nc.sync.dma_start(table_words[:], x_words[0].rearrange("p n t -> p (n t)").bitcast(I32))
+        for q in range(4):
+            nc.scalar.dma_start(table_scales[32 * q : 32 * q + 4, :].bitcast(I32), x_scales[0, 4 * q : 4 * q + 4, :].bitcast(I32))
+        n2_list = load_list(n2, "n2_list")
+        n3_list = load_list(n3, "n3_list")
+        w1_parts = [load_weight(w1, slice(h * H // 2, (h + 1) * H // 2), "w1_raw%d" % h) for h in range(2)]
+        gb_cols = load_gain(gb, "gb_cols")
+        ga_cols = load_gain(ga, "ga_cols")
+        n1_list = load_list(n1, "n1_list")
+        n4_list = load_list(n4, "n4_list")
+        pages = []
+        for c in range(CHUNKS):
+            page = keep.tile([P, U], F32, name="page%d" % c)
+            nc.sync.dma_start(page[:], mem[c * P : (c + 1) * P, :])
+            pages.append(page)
+
+        b_rows = []
+        for t in range(PACK):
+            row = keep.tile([P, 2 * V], F32, name="b_row%d" % t)
+            nc.gpsimd.memset(row[:, V:], 0.0)
+            b_rows.append(row)
+
+        def pick_scales(entries, width, name):
+            picked = keep.tile([P, width], U8, name=name, align_bytes=64)
+            nc.vector.tensor_copy(picked[:], table_scales[:].indirect(entries[:]))
+            return picked
+
+        def pick_words(entries, width, name):
+            picked = keep.tile([P, width], U32, name=name, align_bytes=64)
+            nc.vector.tensor_copy(picked[:], table_words[:].bitcast(U32).indirect(entries[:]))
+            return picked
+
+        two_scales = pick_scales(two_list, V, "two_scales")
+        w2_mx = quantize_weight(w2_parts, "w2")
+        offs_scales = pick_scales(offs_list, S, "offs_scales")
+        two_words = pick_words(two_list, V, "two_words")
+        offs_words = pick_words(offs_list, S, "offs_words")
+
+        b_banks = [psum.tile([P, 2, V], F32, name="b_bank%d" % u) for u in range(2)]
+        pa = keep.tile([P, PACK, V], F32, name="pa")
+        pb = keep.tile([P, PACK, V], F32, name="pb")
+        for t in range(PACK):
+            product(b_banks[t // 2][:, t % 2, :], w2_mx, slice(t * P, (t + 1) * P), (two_words, two_scales))
+        for t in range(PACK):
+            nc.scalar.copy(b_rows[t][:, :V], b_banks[t // 2][:, t % 2, :])
+        for t in range(PACK):
+            nc.scalar.activation(pa[:, t, :], b_rows[t][:].indirect(n2_list[:]), ACT.Copy)
+            nc.scalar.activation(pb[:, t, :], b_rows[t][:].indirect(n3_list[:]), ACT.Copy)
+
+        w1_mx = quantize_weight(w1_parts, "w1")
+        a_rows = []
+        for t in range(PACK):
+            bank = psum.tile([P, S], F32, name="a_bank%d" % t)
+            product(bank[:], w1_mx, slice(t * P, (t + 1) * P), (offs_words, offs_scales))
+            row = keep.tile([P, S], F32, name="a_row%d" % t)
+            nc.vector.tensor_copy(row[:], bank[:])
+            a_rows.append(row)
+
+        members = []
+        for c in range(CHUNKS):
+            pairs = keep.tile([P, PACK, 2 * P], F32, name="pairs%d" % c)
+            for t in range(PACK):
+                nc.scalar.activation(pairs[:, t, :], a_rows[t][:].indirect(n1_list[:, 16 * c : 16 * (c + 1)]), ACT.Copy)
+            members.append(pairs[:].rearrange("p t (j e) -> p (t j) e", e=2))
+
+        high = keep.tile([P, PACK, V], F32, name="high")
+        low = keep.tile([P, PACK, V], F32, name="low")
+        top = keep.tile([P, PACK, V], F32, name="top")
+        bottom = keep.tile([P, PACK, V], F32, name="bottom")
+        spread = keep.tile([P, PACK, V], F32, name="spread")
+        for u in range(2):
+            ts = slice(2 * u, 2 * u + 2)
+            nc.vector.tensor_tensor(high[:, ts, :], pa[:, ts, :], pb[:, ts, :], ALU.max)
+            nc.vector.tensor_tensor(low[:, ts, :], pa[:, ts, :], pb[:, ts, :], ALU.min)
+            nc.vector.tensor_tensor(top[:, ts, :], b_banks[u][:], high[:, ts, :], ALU.max)
+            nc.vector.tensor_tensor(bottom[:, ts, :], b_banks[u][:], low[:, ts, :], ALU.min)
+        for u in range(2):
+            ts = slice(2 * u, 2 * u + 2)
+            nc.vector.scalar_tensor_tensor(spread[:, ts, :], bottom[:, ts, :], -0.5, top[:, ts, :], ALU.mult, ALU.add)
+        z2_rounded = keep.tile([P, V, PACK], BF16, name="z2_rounded", align_bytes=64)
+        nc.vector.tensor_tensor(
+            z2_rounded[:].rearrange("p (c i) t -> p c t i", i=LINE),
+            spread[:].rearrange("p t (c i) -> p c t i", i=LINE),
+            gb_cols[:].unsqueeze(1).unsqueeze(3).to_broadcast([P, V // LINE, PACK, LINE]),
+            ALU.mult,
+        )
+        z2_mx = quantize(z2_rounded[:].rearrange("p v t -> p (v t)"), V, "z2")
+
+        for c in range(CHUNKS):
+            cols = slice(c * P, (c + 1) * P)
+            larger = keep.tile([P, PACK, P], F32, name="larger%d" % c)
+            smaller = keep.tile([P, PACK, P], F32, name="smaller%d" % c)
+            gate = keep.tile([P, PACK, P], F32, name="gate%d" % c)
+            rise = keep.tile([P, PACK, P], F32, name="rise%d" % c)
+            z_exact = keep.tile([P, PACK, P], F32, name="z_exact%d" % c)
+            nc.vector.tensor_tensor(larger[:].rearrange("p t j -> p (t j)"), members[c][:, :, 0], members[c][:, :, 1], ALU.max)
+            nc.scalar.activation(gate[:], larger[:], ACT.Sigmoid)
+            nc.vector.tensor_tensor(smaller[:].rearrange("p t j -> p (t j)"), members[c][:, :, 0], members[c][:, :, 1], ALU.min)
+            for t in range(PACK):
+                nc.vector.tensor_tensor(rise[:, t, :], a_rows[t][:, cols], smaller[:, t, :], ALU.subtract)
+            for t in range(PACK):
+                nc.vector.scalar_tensor_tensor(z_exact[:, t, :], rise[:, t, :], ga_cols[:, t : t + 1], gate[:, t, :], ALU.mult, ALU.mult)
+            z_rounded = keep.tile([P, P, PACK], BF16, name="z_rounded%d" % c, align_bytes=64)
+            nc.vector.tensor_copy(
+                z_rounded[:].rearrange("p (c i) t -> p c t i", i=LINE),
+                z_exact[:].rearrange("p t (c i) -> p c t i", i=LINE),
+            )
+            z_mx = quantize(z_rounded[:].rearrange("p j t -> p (j t)"), P, "z_chunk%d" % c)
+            s_bank = psum.tile([P, V], F32, name="s_bank%d" % (c % 2))
+            product(s_bank[:], z_mx, slice(0, P), z2_mx)
+            scores = keep.tile([P, V], F32, name="scores%d" % c)
+            nc.scalar.activation(scores[:], s_bank[:], ACT.Copy, scale=0.0625)
+            nc.scalar.activation(pages[c][:].indirect(n4_list[:]), scores[:], ACT.Copy)
+            nc.sync.dma_start(out[c * P : (c + 1) * P, :], pages[c][:])

@@ -19,6 +19,9 @@ P = 128
 PACK = 4
 LINE = 4
 CHUNKS = S // P
+HALF = S // 2
+SPARE = 16
+W2_ON_VECTOR = 128
 
 
 def tile_picked_kqghardrangepage_none_p_kernel(tc, x_words, x_scales, w1, w2, ga, gb, mem, offs, two, n1, n2, n3, n4, out):
@@ -43,19 +46,21 @@ def tile_picked_kqghardrangepage_none_p_kernel(tc, x_words, x_scales, w1, w2, ga
             return tile
 
         def quantize(rounded, width, name):
-            codes = keep.tile([P, width], U32, name=name + "_codes", align_bytes=64)
+            codes = keep.tile([P, width], U32, name="codes", tag=name + "_codes", align_bytes=64)
             scales = keep.tile([P, width], U8, name=name + "_scales", align_bytes=64)
             nc.vector.quantize_mx(out=codes[:].bitcast(FP8X4), scales=scales[:], in_=rounded)
             return codes, scales
 
         def quantize_weight(parts, name):
             dealt = keep.tile([P, PACK, P, PACK], BF16, name=name + "_dealt", align_bytes=64)
-            share = P // len(parts)
-            for i, part in enumerate(parts):
-                nc.vector.tensor_copy(
-                    out=dealt[:, :, i * share : (i + 1) * share, :].rearrange("p t m j -> p m j t"),
-                    in_=part[:].rearrange("p j (m t) -> p m j t", t=PACK),
+            first = 0
+            for part, copy in parts:
+                count = part.shape[2] // PACK
+                copy(
+                    dealt[:, :, first : first + count, :].rearrange("p t m j -> p m j t"),
+                    part.rearrange("p j (m t) -> p m j t", t=PACK),
                 )
+                first = first + count
             return quantize(dealt[:].rearrange("p t m j -> p (t m j)"), H, name)
 
         def product(acc, left, left_cols, right):
@@ -70,14 +75,14 @@ def tile_picked_kqghardrangepage_none_p_kernel(tc, x_words, x_scales, w1, w2, ga
             )
 
         table_scales = keep.tile([P, T], U8, name="table_scales")
-        nc.vector.memset(table_scales[:].bitcast(I32), 0)
+        nc.gpsimd.memset(table_scales[:].bitcast(I32), 0)
+        w2_raw = load_weight(w2, slice(0, H), "w2_raw")
+        for q in range(4):
+            nc.sync.dma_start(table_scales[32 * q : 32 * q + 4, :].bitcast(I32), x_scales[0, 4 * q : 4 * q + 4, :].bitcast(I32))
         two_list = load_list(two, "two_list")
         offs_list = load_list(offs, "offs_list")
-        w2_parts = [load_weight(w2, slice(0, H), "w2_raw")]
         table_words = keep.tile([P, T], I32, name="table_words")
         nc.sync.dma_start(table_words[:], x_words[0].rearrange("p n t -> p (n t)").bitcast(I32))
-        for q in range(4):
-            nc.scalar.dma_start(table_scales[32 * q : 32 * q + 4, :].bitcast(I32), x_scales[0, 4 * q : 4 * q + 4, :].bitcast(I32))
         n2_list = load_list(n2, "n2_list")
         n3_list = load_list(n3, "n3_list")
         w1_parts = [load_weight(w1, slice(h * H // 2, (h + 1) * H // 2), "w1_raw%d" % h) for h in range(2)]
@@ -94,8 +99,15 @@ def tile_picked_kqghardrangepage_none_p_kernel(tc, x_words, x_scales, w1, w2, ga
         b_rows = []
         for t in range(PACK):
             row = keep.tile([P, 2 * V], F32, name="b_row%d" % t)
-            nc.gpsimd.memset(row[:, V:], 0.0)
+            nc.vector.memset(row[:, V:], 0.0)
             b_rows.append(row)
+        a_rows = []
+        for t in range(PACK):
+            row = keep.tile([P, S + SPARE], F32, name="a_row%d" % t)
+            nc.vector.memset(row[:, S:], 0.0)
+            a_rows.append(row)
+        warm = keep.tile([P, 1], F32, name="warm")
+        nc.scalar.activation(warm[:], b_rows[0][:, V : V + 1], ACT.Sigmoid)
 
         def pick_scales(entries, width, name):
             picked = keep.tile([P, width], U8, name=name, align_bytes=64)
@@ -103,14 +115,14 @@ def tile_picked_kqghardrangepage_none_p_kernel(tc, x_words, x_scales, w1, w2, ga
             return picked
 
         def pick_words(entries, width, name):
-            picked = keep.tile([P, width], U32, name=name, align_bytes=64)
+            picked = keep.tile([P, width], U32, name="picked", tag=name, align_bytes=64)
             nc.vector.tensor_copy(picked[:], table_words[:].bitcast(U32).indirect(entries[:]))
             return picked
 
+        w2_mx = quantize_weight(((w2_raw[:, :, :W2_ON_VECTOR], nc.vector.tensor_copy), (w2_raw[:, :, W2_ON_VECTOR:], nc.scalar.copy)), "w2")
         two_scales = pick_scales(two_list, V, "two_scales")
-        w2_mx = quantize_weight(w2_parts, "w2")
-        offs_scales = pick_scales(offs_list, S, "offs_scales")
         two_words = pick_words(two_list, V, "two_words")
+        offs_scales = pick_scales(offs_list, S, "offs_scales")
         offs_words = pick_words(offs_list, S, "offs_words")
 
         b_banks = [psum.tile([P, 2, V], F32, name="b_bank%d" % u) for u in range(2)]
@@ -124,68 +136,114 @@ def tile_picked_kqghardrangepage_none_p_kernel(tc, x_words, x_scales, w1, w2, ga
             nc.scalar.activation(pa[:, t, :], b_rows[t][:].indirect(n2_list[:]), ACT.Copy)
             nc.scalar.activation(pb[:, t, :], b_rows[t][:].indirect(n3_list[:]), ACT.Copy)
 
-        w1_mx = quantize_weight(w1_parts, "w1")
-        a_rows = []
+        w1_mx = quantize_weight([(part[:], nc.vector.tensor_copy) for part in w1_parts], "w1")
         for t in range(PACK):
             bank = psum.tile([P, S], F32, name="a_bank%d" % t)
             product(bank[:], w1_mx, slice(t * P, (t + 1) * P), (offs_words, offs_scales))
-            row = keep.tile([P, S], F32, name="a_row%d" % t)
-            nc.vector.tensor_copy(row[:], bank[:])
-            a_rows.append(row)
+            nc.vector.tensor_copy(a_rows[t][:, :S], bank[:])
 
-        members = []
-        for c in range(CHUNKS):
-            pairs = keep.tile([P, PACK, 2 * P], F32, name="pairs%d" % c)
-            for t in range(PACK):
-                nc.scalar.activation(pairs[:, t, :], a_rows[t][:].indirect(n1_list[:, 16 * c : 16 * (c + 1)]), ACT.Copy)
-            members.append(pairs[:].rearrange("p t (j e) -> p (t j) e", e=2))
+        def fetch_members(h, u):
+            pairs = keep.tile([P, 2, 2 * HALF], F32, name="pairs", bufs=2)
+            entries = n1_list[:, h * HALF // 8 : (h + 1) * HALF // 8]
+            for e in range(2):
+                nc.scalar.activation(pairs[:, e, :], a_rows[2 * u + e][:].indirect(entries), ACT.Copy)
+            members[h, u] = pairs[:].rearrange("p t (j e) -> p (t j) e", e=2)
 
-        high = keep.tile([P, PACK, V], F32, name="high")
-        low = keep.tile([P, PACK, V], F32, name="low")
-        top = keep.tile([P, PACK, V], F32, name="top")
-        bottom = keep.tile([P, PACK, V], F32, name="bottom")
-        spread = keep.tile([P, PACK, V], F32, name="spread")
-        for u in range(2):
-            ts = slice(2 * u, 2 * u + 2)
-            nc.vector.tensor_tensor(high[:, ts, :], pa[:, ts, :], pb[:, ts, :], ALU.max)
-            nc.vector.tensor_tensor(low[:, ts, :], pa[:, ts, :], pb[:, ts, :], ALU.min)
-            nc.vector.tensor_tensor(top[:, ts, :], b_banks[u][:], high[:, ts, :], ALU.max)
-            nc.vector.tensor_tensor(bottom[:, ts, :], b_banks[u][:], low[:, ts, :], ALU.min)
-        for u in range(2):
-            ts = slice(2 * u, 2 * u + 2)
-            nc.vector.scalar_tensor_tensor(spread[:, ts, :], bottom[:, ts, :], -0.5, top[:, ts, :], ALU.mult, ALU.add)
-        z2_rounded = keep.tile([P, V, PACK], BF16, name="z2_rounded", align_bytes=64)
-        nc.vector.tensor_tensor(
-            z2_rounded[:].rearrange("p (c i) t -> p c t i", i=LINE),
-            spread[:].rearrange("p t (c i) -> p c t i", i=LINE),
-            gb_cols[:].unsqueeze(1).unsqueeze(3).to_broadcast([P, V // LINE, PACK, LINE]),
-            ALU.mult,
-        )
-        z2_mx = quantize(z2_rounded[:].rearrange("p v t -> p (v t)"), V, "z2")
+        members, gates, smallers = {}, {}, {}
 
-        for c in range(CHUNKS):
-            cols = slice(c * P, (c + 1) * P)
-            larger = keep.tile([P, PACK, P], F32, name="larger%d" % c)
-            smaller = keep.tile([P, PACK, P], F32, name="smaller%d" % c)
-            gate = keep.tile([P, PACK, P], F32, name="gate%d" % c)
-            rise = keep.tile([P, PACK, P], F32, name="rise%d" % c)
-            z_exact = keep.tile([P, PACK, P], F32, name="z_exact%d" % c)
-            nc.vector.tensor_tensor(larger[:].rearrange("p t j -> p (t j)"), members[c][:, :, 0], members[c][:, :, 1], ALU.max)
+        def gate_of_larger(h, u):
+            larger = keep.tile([P, 2, HALF], F32, name="larger%d%d" % (h, u))
+            gate = keep.tile([P, 2, HALF], F32, name="gate%d%d" % (h, u))
+            nc.vector.tensor_tensor(larger[:].rearrange("p t j -> p (t j)"), members[h, u][:, :, 0], members[h, u][:, :, 1], ALU.max)
             nc.scalar.activation(gate[:], larger[:], ACT.Sigmoid)
-            nc.vector.tensor_tensor(smaller[:].rearrange("p t j -> p (t j)"), members[c][:, :, 0], members[c][:, :, 1], ALU.min)
-            for t in range(PACK):
-                nc.vector.tensor_tensor(rise[:, t, :], a_rows[t][:, cols], smaller[:, t, :], ALU.subtract)
-            for t in range(PACK):
-                nc.vector.scalar_tensor_tensor(z_exact[:, t, :], rise[:, t, :], ga_cols[:, t : t + 1], gate[:, t, :], ALU.mult, ALU.mult)
+            gates[h, u] = gate
+
+        def take_smaller(h, u):
+            smaller = keep.tile([P, 2, HALF], F32, name="smaller%d%d" % (h, u))
+            nc.vector.tensor_tensor(smaller[:].rearrange("p t j -> p (t j)"), members[h, u][:, :, 0], members[h, u][:, :, 1], ALU.min)
+            smallers[h, u] = smaller
+
+        rise = [keep.tile([P, PACK, HALF], F32, name="rise%d" % h) for h in range(2)]
+        z_exact = [keep.tile([P, PACK, HALF], F32, name="z_exact%d" % h) for h in range(2)]
+
+        def weigh_z(h, planes, cols):
+            in_a = slice(h * HALF + cols.start, h * HALF + cols.stop)
+            for t in planes:
+                smaller = smallers[h, t // 2]
+                nc.vector.tensor_tensor(rise[h][:, t, cols], a_rows[t][:, in_a], smaller[:, t % 2, cols], ALU.subtract)
+            for t in planes:
+                gate = gates[h, t // 2]
+                nc.vector.scalar_tensor_tensor(z_exact[h][:, t, cols], rise[h][:, t, cols], ga_cols[:, t : t + 1], gate[:, t % 2, cols], ALU.mult, ALU.mult)
+
+        def round_z(c):
             z_rounded = keep.tile([P, P, PACK], BF16, name="z_rounded%d" % c, align_bytes=64)
             nc.vector.tensor_copy(
                 z_rounded[:].rearrange("p (c i) t -> p c t i", i=LINE),
-                z_exact[:].rearrange("p t (c i) -> p c t i", i=LINE),
+                z_exact[c // 2][:, :, c % 2 * P : (c % 2 + 1) * P].rearrange("p t (c i) -> p c t i", i=LINE),
             )
+            return z_rounded
+
+        def write_page(c, z_rounded, z2_mx):
             z_mx = quantize(z_rounded[:].rearrange("p j t -> p (j t)"), P, "z_chunk%d" % c)
             s_bank = psum.tile([P, V], F32, name="s_bank%d" % (c % 2))
             product(s_bank[:], z_mx, slice(0, P), z2_mx)
             scores = keep.tile([P, V], F32, name="scores%d" % c)
-            nc.scalar.activation(scores[:], s_bank[:], ACT.Copy, scale=0.0625)
+            if c < 2:
+                nc.scalar.activation(scores[:], s_bank[:], ACT.Copy, scale=0.0625)
+            else:
+                nc.vector.tensor_scalar(scores[:], s_bank[:], 0.0625, None, ALU.mult)
             nc.scalar.activation(pages[c][:].indirect(n4_list[:]), scores[:], ACT.Copy)
             nc.sync.dma_start(out[c * P : (c + 1) * P, :], pages[c][:])
+
+        spread = keep.tile([P, PACK, V], F32, name="spread")
+
+        def order_looked_up(u):
+            ts = slice(2 * u, 2 * u + 2)
+            both = keep.tile([P, 2, 2, V], F32, name="both", tag=("w1_codes", "offs_words")[u], align_bytes=64)
+            nc.vector.tensor_tensor(both[:, 0], pa[:, ts, :], pb[:, ts, :], ALU.max)
+            nc.vector.tensor_tensor(both[:, 1], pa[:, ts, :], pb[:, ts, :], ALU.min)
+            return both
+
+        def order_three(u, both):
+            top = keep.tile([P, 2, V], F32, name="top%d" % u)
+            bottom = keep.tile([P, 2, V], F32, name="bottom%d" % u)
+            nc.vector.tensor_tensor(top[:], b_banks[u][:], both[:, 0], ALU.max)
+            nc.vector.tensor_tensor(bottom[:], b_banks[u][:], both[:, 1], ALU.min)
+            return top, bottom
+
+        def finish_spread(u, top, bottom):
+            nc.vector.scalar_tensor_tensor(spread[:, 2 * u : 2 * u + 2, :], bottom[:], -0.5, top[:], ALU.mult, ALU.add)
+
+        def quantize_z2():
+            z2_rounded = keep.tile([P, V, PACK], BF16, name="z2_rounded", align_bytes=64)
+            nc.vector.tensor_tensor(
+                z2_rounded[:].rearrange("p (c i) t -> p c t i", i=LINE),
+                spread[:].rearrange("p t (c i) -> p c t i", i=LINE),
+                gb_cols[:].unsqueeze(1).unsqueeze(3).to_broadcast([P, V // LINE, PACK, LINE]),
+                ALU.mult,
+            )
+            return z2_rounded
+
+        fetch_members(0, 0)
+        fetch_members(0, 1)
+        for u in range(2):
+            finish_spread(u, *order_three(u, order_looked_up(u)))
+        z2_rounded = quantize_z2()
+        gate_of_larger(0, 0)
+        take_smaller(0, 0)
+        z2_mx = quantize(z2_rounded[:].rearrange("p v t -> p (v t)"), V, "z2")
+        fetch_members(1, 0)
+        gate_of_larger(0, 1)
+        take_smaller(0, 1)
+        fetch_members(1, 1)
+        weigh_z(0, range(PACK), slice(0, HALF))
+        gate_of_larger(1, 0)
+        rounded = [round_z(0), round_z(1)]
+        write_page(0, rounded[0], z2_mx)
+        gate_of_larger(1, 1)
+        write_page(1, rounded[1], z2_mx)
+        take_smaller(1, 0)
+        take_smaller(1, 1)
+        for c in range(2):
+            weigh_z(1, range(PACK), slice(c * P, (c + 1) * P))
+            write_page(2 + c, round_z(2 + c), z2_mx)

@@ -21,7 +21,6 @@ LINE = 4
 CHUNKS = S // P
 HALF = S // 2
 SPARE = 16
-W2_ON_VECTOR = 128
 
 
 def tile_picked_kqghardrangepage_none_p_kernel(tc, x_words, x_scales, w1, w2, ga, gb, mem, offs, two, n1, n2, n3, n4, out):
@@ -41,27 +40,21 @@ def tile_picked_kqghardrangepage_none_p_kernel(tc, x_words, x_scales, w1, w2, ga
             return tile
 
         def load_weight(src, cols, name):
-            tile = keep.tile([P, PACK, cols.stop - cols.start], F32, name=name)
+            tile = keep.tile([P, PACK, cols.stop - cols.start], F32, name="raw", tag=name)
             nc.sync.dma_start(tile[:], src[:, cols].rearrange("(p j) c -> p j c", j=PACK))
             return tile
 
-        def quantize(rounded, width, name):
+        def quantize(rounded, width, name, scales_tag=None):
             codes = keep.tile([P, width], U32, name="codes", tag=name + "_codes", align_bytes=64)
-            scales = keep.tile([P, width], U8, name=name + "_scales", align_bytes=64)
+            scales = keep.tile([P, width], U8, name="scales", tag=scales_tag or name + "_scales", align_bytes=64)
             nc.vector.quantize_mx(out=codes[:].bitcast(FP8X4), scales=scales[:], in_=rounded)
             return codes, scales
 
-        def quantize_weight(parts, name):
-            dealt = keep.tile([P, PACK, P, PACK], BF16, name=name + "_dealt", align_bytes=64)
-            first = 0
-            for part, copy in parts:
-                count = part.shape[2] // PACK
-                copy(
-                    dealt[:, :, first : first + count, :].rearrange("p t m j -> p m j t"),
-                    part.rearrange("p j (m t) -> p m j t", t=PACK),
-                )
-                first = first + count
-            return quantize(dealt[:].rearrange("p t m j -> p (t m j)"), H, name)
+        def deal(copy, dealt, raw):
+            copy(dealt.rearrange("p t m j -> p m j t"), raw.rearrange("p j (m t) -> p m j t", t=PACK))
+
+        def quantize_pair(dealt, name):
+            return quantize(dealt.rearrange("p t m j -> p (t m j)"), 2 * P, name)
 
         def product(acc, left, left_cols, right):
             nc.tensor.matmul_mx(
@@ -74,8 +67,8 @@ def tile_picked_kqghardrangepage_none_p_kernel(tc, x_words, x_scales, w1, w2, ga
                 stop=True,
             )
 
-        table_scales = keep.tile([P, T], U8, name="table_scales")
-        nc.gpsimd.memset(table_scales[:].bitcast(I32), 0)
+        table_scales = keep.tile([P, T], U8, name="table_scales", align_bytes=64)
+        nc.vector.memset(table_scales[:].bitcast(I32), 0)
         w2_raw = load_weight(w2, slice(0, H), "w2_raw")
         for q in range(4):
             nc.sync.dma_start(table_scales[32 * q : 32 * q + 4, :].bitcast(I32), x_scales[0, 4 * q : 4 * q + 4, :].bitcast(I32))
@@ -114,32 +107,37 @@ def tile_picked_kqghardrangepage_none_p_kernel(tc, x_words, x_scales, w1, w2, ga
             nc.vector.tensor_copy(picked[:], table_scales[:].indirect(entries[:]))
             return picked
 
-        def pick_words(entries, width, name):
-            picked = keep.tile([P, width], U32, name="picked", tag=name, align_bytes=64)
-            nc.vector.tensor_copy(picked[:], table_words[:].bitcast(U32).indirect(entries[:]))
+        def pick_words(entries, picked):
+            nc.vector.tensor_copy(picked, table_words[:].bitcast(U32).indirect(entries[:]))
             return picked
 
-        w2_mx = quantize_weight(((w2_raw[:, :, :W2_ON_VECTOR], nc.vector.tensor_copy), (w2_raw[:, :, W2_ON_VECTOR:], nc.scalar.copy)), "w2")
         two_scales = pick_scales(two_list, V, "two_scales")
-        two_words = pick_words(two_list, V, "two_words")
         offs_scales = pick_scales(offs_list, S, "offs_scales")
-        offs_words = pick_words(offs_list, S, "offs_words")
+        w2_dealt = keep.tile([P, PACK, P, PACK], BF16, name="w2_dealt", align_bytes=64)
+        deal(nc.scalar.copy, w2_dealt[:], w2_raw[:])
+        w2_mx = quantize(w2_dealt[:].rearrange("p t m j -> p (t m j)"), H, "w2", "table_scales")
+        w1_dealt = keep.tile([P, PACK, P, PACK], BF16, name="w1_dealt", align_bytes=64)
+        for h in range(2):
+            deal(nc.scalar.copy, w1_dealt[:, :, h * P // 2 : (h + 1) * P // 2, :], w1_parts[h][:])
+        picked_words = keep.tile([P, V + S], U32, name="picked_words", tag="w2_dealt", align_bytes=64)
+        two_words = pick_words(two_list, picked_words[:, :V])
+        offs_words = pick_words(offs_list, picked_words[:, V:])
 
         b_banks = [psum.tile([P, 2, V], F32, name="b_bank%d" % u) for u in range(2)]
-        pa = keep.tile([P, PACK, V], F32, name="pa")
-        pb = keep.tile([P, PACK, V], F32, name="pb")
+        looked_up = keep.tile([P, 2, PACK, V], F32, name="looked_up", tag="w1_raw1")
+        pa, pb = looked_up[:, 0], looked_up[:, 1]
         for t in range(PACK):
             product(b_banks[t // 2][:, t % 2, :], w2_mx, slice(t * P, (t + 1) * P), (two_words, two_scales))
         for t in range(PACK):
-            nc.scalar.copy(b_rows[t][:, :V], b_banks[t // 2][:, t % 2, :])
+            nc.vector.tensor_copy(b_rows[t][:, :V], b_banks[t // 2][:, t % 2, :])
         for t in range(PACK):
             nc.scalar.activation(pa[:, t, :], b_rows[t][:].indirect(n2_list[:]), ACT.Copy)
             nc.scalar.activation(pb[:, t, :], b_rows[t][:].indirect(n3_list[:]), ACT.Copy)
 
-        w1_mx = quantize_weight([(part[:], nc.vector.tensor_copy) for part in w1_parts], "w1")
+        w1_mx = [quantize_pair(w1_dealt[:, 2 * u : 2 * u + 2], "w1_%d" % u) for u in range(2)]
         for t in range(PACK):
             bank = psum.tile([P, S], F32, name="a_bank%d" % t)
-            product(bank[:], w1_mx, slice(t * P, (t + 1) * P), (offs_words, offs_scales))
+            product(bank[:], w1_mx[t // 2], slice(t % 2 * P, (t % 2 + 1) * P), (offs_words, offs_scales))
             nc.vector.tensor_copy(a_rows[t][:, :S], bank[:])
 
         def fetch_members(h, u):
@@ -199,7 +197,7 @@ def tile_picked_kqghardrangepage_none_p_kernel(tc, x_words, x_scales, w1, w2, ga
 
         def order_looked_up(u):
             ts = slice(2 * u, 2 * u + 2)
-            both = keep.tile([P, 2, 2, V], F32, name="both", tag=("w1_codes", "offs_words")[u], align_bytes=64)
+            both = keep.tile([P, 2, 2, V], F32, name="both", tag=("w1_1_codes", "w2_dealt")[u], align_bytes=64)
             nc.vector.tensor_tensor(both[:, 0], pa[:, ts, :], pb[:, ts, :], ALU.max)
             nc.vector.tensor_tensor(both[:, 1], pa[:, ts, :], pb[:, ts, :], ALU.min)
             return both

from contextlib import ExitStack

import concourse.mybir as mybir

K, T, S, V, H, U = 512, 2048, 512, 256, 512, 1024
FLOPS = 2 * K * H * S + 2 * K * H * V + 2 * H * S * V

F32 = mybir.dt.float32
BF16 = mybir.dt.bfloat16
I32 = mybir.dt.int32
U32 = mybir.dt.uint32
U16 = mybir.dt.uint16
U8 = mybir.dt.uint8
FP8X4 = mybir.dt.float8_e4m3fn_x4
ALU = mybir.AluOpType
ACT = mybir.ActivationFunctionType

P = 128
PACK = 4
LINE = 4
CHUNKS = S // P
HALF = S // 2
SPARE = 16


def tile_picked_kqghardrangepage_none_p_kernel(tc, x_words, x_scales, w1, w2, ga, gb, mem, offs, two, n1, n2, n3, n4, out):
    nc = tc.nc
    with ExitStack() as ctx:
        keep = ctx.enter_context(tc.tile_pool(name="keep", bufs=1))
        psum = ctx.enter_context(tc.psum_pool(name="psum", bufs=1))

        def load_list(src, name):
            tile = keep.tile(list(src.shape), U16, name=name)
            nc.sync.dma_start(tile[:], src)
            return tile

        def load_gain(src, name):
            tile = keep.tile([P, PACK], F32, name=name)
            nc.sync.dma_start(tile[:], src.rearrange("(p t) o -> p (t o)", t=PACK))
            return tile

        def load_weight(src, cols, name):
            tile = keep.tile([P, PACK, cols.stop - cols.start], F32, name="raw", tag=name)
            nc.sync.dma_start(tile[:], src[:, cols].rearrange("(p j) c -> p j c", j=PACK))
            return tile

        def quantize(rounded, width, name, scales_tag=None):
            codes = keep.tile([P, width], U32, name="codes", tag=name + "_codes", align_bytes=64)
            scales = keep.tile([P, width], U8, name="scales", tag=scales_tag or name + "_scales", align_bytes=64)
            nc.vector.quantize_mx(out=codes[:].bitcast(FP8X4), scales=scales[:], in_=rounded)
            return codes, scales

        def deal(copy, dealt, raw):
            copy(dealt.rearrange("p t m j -> p m j t"), raw.rearrange("p j (m t) -> p m j t", t=PACK))

        def quantize_pair(dealt, name):
            return quantize(dealt.rearrange("p t m j -> p (t m j)"), 2 * P, name)

        def product(acc, left, left_cols, right):
            nc.tensor.matmul_mx(
                out=acc,
                lhsT=left[0][:, left_cols].bitcast(FP8X4),
                lhsT_scale=left[1][:, left_cols],
                rhs=right[0][:].bitcast(FP8X4),
                rhs_scale=right[1][:],
                start=True,
                stop=True,
            )

        table_scales = keep.tile([P, T], U8, name="table_scales", align_bytes=64)
        nc.vector.memset(table_scales[:].bitcast(I32), 0)
        w2_raw = load_weight(w2, slice(0, H), "w2_raw")
        for q in range(4):
            nc.sync.dma_start(table_scales[32 * q : 32 * q + 4, :].bitcast(I32), x_scales[0, 4 * q : 4 * q + 4, :].bitcast(I32))
        two_list = load_list(two, "two_list")
        offs_list = load_list(offs, "offs_list")
        table_words = keep.tile([P, T], I32, name="table_words")
        nc.sync.dma_start(table_words[:], x_words[0].rearrange("p n t -> p (n t)").bitcast(I32))
        n2_list = load_list(n2, "n2_list")
        n3_list = load_list(n3, "n3_list")
        w1_parts = [load_weight(w1, slice(h * H // 2, (h + 1) * H // 2), "w1_raw%d" % h) for h in range(2)]
        gb_cols = load_gain(gb, "gb_cols")
        ga_cols = load_gain(ga, "ga_cols")
        n1_list = load_list(n1, "n1_list")
        n4_list = load_list(n4, "n4_list")
        pages = []
        for c in range(CHUNKS):
            page = keep.tile([P, U], F32, name="page%d" % c)
            nc.sync.dma_start(page[:], mem[c * P : (c + 1) * P, :])
            pages.append(page)

        b_rows = []
        for t in range(PACK):
            row = keep.tile([P, 2 * V], F32, name="b_row%d" % t)
            nc.vector.memset(row[:, V:], 0.0)
            b_rows.append(row)
        a_rows = []
        for t in range(PACK):
            row = keep.tile([P, S + SPARE], F32, name="a_row%d" % t)
            nc.vector.memset(row[:, S:], 0.0)
            a_rows.append(row)
        warm = keep.tile([P, 1], F32, name="warm")
        nc.scalar.activation(warm[:], b_rows[0][:, V : V + 1], ACT.Sigmoid)

        def pick_scales(entries, width, name):
            picked = keep.tile([P, width], U8, name=name, align_bytes=64)
            nc.vector.tensor_copy(picked[:], table_scales[:].indirect(entries[:]))
            return picked

        def pick_words(entries, picked):
            nc.vector.tensor_copy(picked, table_words[:].bitcast(U32).indirect(entries[:]))
            return picked

        two_scales = pick_scales(two_list, V, "two_scales")
        offs_scales = pick_scales(offs_list, S, "offs_scales")
        w2_dealt = keep.tile([P, PACK, P, PACK], BF16, name="w2_dealt", align_bytes=64)
        deal(nc.scalar.copy, w2_dealt[:], w2_raw[:])
        w2_mx = quantize(w2_dealt[:].rearrange("p t m j -> p (t m j)"), H, "w2", "table_scales")
        w1_dealt = keep.tile([P, PACK, P, PACK], BF16, name="w1_dealt", align_bytes=64)
        for h in range(2):
            deal(nc.scalar.copy, w1_dealt[:, :, h * P // 2 : (h + 1) * P // 2, :], w1_parts[h][:])
        picked_words = keep.tile([P, V + S], U32, name="picked_words", tag="w2_dealt", align_bytes=64)
        two_words = pick_words(two_list, picked_words[:, :V])
        offs_words = pick_words(offs_list, picked_words[:, V:])

        b_banks = [psum.tile([P, 2, V], F32, name="b_bank%d" % u) for u in range(2)]
        looked_up = keep.tile([P, 2, PACK, V], F32, name="looked_up", tag="w1_raw1")
        pa, pb = looked_up[:, 0], looked_up[:, 1]
        for t in range(PACK):
            product(b_banks[t // 2][:, t % 2, :], w2_mx, slice(t * P, (t + 1) * P), (two_words, two_scales))
        for t in range(PACK):
            nc.vector.tensor_copy(b_rows[t][:, :V], b_banks[t // 2][:, t % 2, :])
        for t in range(PACK):
            nc.scalar.activation(pa[:, t, :], b_rows[t][:].indirect(n2_list[:]), ACT.Copy)
            nc.scalar.activation(pb[:, t, :], b_rows[t][:].indirect(n3_list[:]), ACT.Copy)

        w1_mx = [quantize_pair(w1_dealt[:, 2 * u : 2 * u + 2], "w1_%d" % u) for u in range(2)]
        for t in range(PACK):
            bank = psum.tile([P, S], F32, name="a_bank%d" % t)
            product(bank[:], w1_mx[t // 2], slice(t % 2 * P, (t % 2 + 1) * P), (offs_words, offs_scales))
            nc.vector.tensor_copy(a_rows[t][:, :S], bank[:])

        def fetch_members(h, u):
            pairs = keep.tile([P, 2, 2 * HALF], F32, name="pairs", bufs=2)
            entries = n1_list[:, h * HALF // 8 : (h + 1) * HALF // 8]
            for e in range(2):
                nc.scalar.activation(pairs[:, e, :], a_rows[2 * u + e][:].indirect(entries), ACT.Copy)
            members[h, u] = pairs[:].rearrange("p t (j e) -> p (t j) e", e=2)

        members, gates, smallers = {}, {}, {}

        def gate_of_larger(h, u):
            larger = keep.tile([P, 2, HALF], F32, name="larger%d%d" % (h, u))
            gate = keep.tile([P, 2, HALF], F32, name="gate%d%d" % (h, u))
            nc.vector.tensor_tensor(larger[:].rearrange("p t j -> p (t j)"), members[h, u][:, :, 0], members[h, u][:, :, 1], ALU.max)
            nc.scalar.activation(gate[:], larger[:], ACT.Sigmoid)
            gates[h, u] = gate

        def take_smaller(h, u):
            smaller = keep.tile([P, 2, HALF], F32, name="smaller%d%d" % (h, u))
            nc.vector.tensor_tensor(smaller[:].rearrange("p t j -> p (t j)"), members[h, u][:, :, 0], members[h, u][:, :, 1], ALU.min)
            smallers[h, u] = smaller

        rise = [keep.tile([P, PACK, HALF], F32, name="rise%d" % h) for h in range(2)]
        z_exact = [keep.tile([P, PACK, HALF], F32, name="z_exact%d" % h) for h in range(2)]

        def weigh_z(h, planes, cols):
            in_a = slice(h * HALF + cols.start, h * HALF + cols.stop)
            for t in planes:
                smaller = smallers[h, t // 2]
                nc.vector.tensor_tensor(rise[h][:, t, cols], a_rows[t][:, in_a], smaller[:, t % 2, cols], ALU.subtract)
            for t in planes:
                gate = gates[h, t // 2]
                nc.vector.scalar_tensor_tensor(z_exact[h][:, t, cols], rise[h][:, t, cols], ga_cols[:, t : t + 1], gate[:, t % 2, cols], ALU.mult, ALU.mult)

        def round_z(c):
            z_rounded = keep.tile([P, P, PACK], BF16, name="z_rounded%d" % c, align_bytes=64)
            nc.vector.tensor_copy(
                z_rounded[:].rearrange("p (c i) t -> p c t i", i=LINE),
                z_exact[c // 2][:, :, c % 2 * P : (c % 2 + 1) * P].rearrange("p t (c i) -> p c t i", i=LINE),
            )
            return z_rounded

        def write_page(c, z_rounded, z2_mx):
            z_mx = quantize(z_rounded[:].rearrange("p j t -> p (j t)"), P, "z_chunk%d" % c)
            s_bank = psum.tile([P, V], F32, name="s_bank%d" % (c % 2))
            product(s_bank[:], z_mx, slice(0, P), z2_mx)
            scores = keep.tile([P, V], F32, name="scores%d" % c)
            if c < 2:
                nc.scalar.activation(scores[:], s_bank[:], ACT.Copy, scale=0.0625)
            else:
                nc.vector.tensor_scalar(scores[:], s_bank[:], 0.0625, None, ALU.mult)
            nc.scalar.activation(pages[c][:].indirect(n4_list[:]), scores[:], ACT.Copy)
            nc.sync.dma_start(out[c * P : (c + 1) * P, :], pages[c][:])

        spread = keep.tile([P, PACK, V], F32, name="spread")

        def order_looked_up(u):
            ts = slice(2 * u, 2 * u + 2)
            both = keep.tile([P, 2, 2, V], F32, name="both", tag=("w1_1_codes", "w2_dealt")[u], align_bytes=64)
            nc.vector.tensor_tensor(both[:, 0], pa[:, ts, :], pb[:, ts, :], ALU.max)
            nc.vector.tensor_tensor(both[:, 1], pa[:, ts, :], pb[:, ts, :], ALU.min)
            return both

        def order_three(u, both):
            top = keep.tile([P, 2, V], F32, name="top%d" % u)
            bottom = keep.tile([P, 2, V], F32, name="bottom%d" % u)
            nc.vector.tensor_tensor(top[:], b_banks[u][:], both[:, 0], ALU.max)
            nc.vector.tensor_tensor(bottom[:], b_banks[u][:], both[:, 1], ALU.min)
            return top, bottom

        def finish_spread(u, top, bottom):
            nc.vector.scalar_tensor_tensor(spread[:, 2 * u : 2 * u + 2, :], bottom[:], -0.5, top[:], ALU.mult, ALU.add)

        def quantize_z2():
            z2_rounded = keep.tile([P, V, PACK], BF16, name="z2_rounded", align_bytes=64)
            nc.vector.tensor_tensor(
                z2_rounded[:].rearrange("p (c i) t -> p c t i", i=LINE),
                spread[:].rearrange("p t (c i) -> p c t i", i=LINE),
                gb_cols[:].unsqueeze(1).unsqueeze(3).to_broadcast([P, V // LINE, PACK, LINE]),
                ALU.mult,
            )
            return z2_rounded

        fetch_members(0, 0)
        fetch_members(0, 1)
        for u in range(2):
            finish_spread(u, *order_three(u, order_looked_up(u)))
        z2_rounded = quantize_z2()
        gate_of_larger(0, 0)
        take_smaller(0, 0)
        z2_mx = quantize(z2_rounded[:].rearrange("p v t -> p (v t)"), V, "z2")
        fetch_members(1, 0)
        gate_of_larger(0, 1)
        take_smaller(0, 1)
        fetch_members(1, 1)
        weigh_z(0, range(PACK), slice(0, HALF))
        gate_of_larger(1, 0)
        rounded = [round_z(0), round_z(1)]
        write_page(0, rounded[0], z2_mx)
        gate_of_larger(1, 1)
        write_page(1, rounded[1], z2_mx)
        take_smaller(1, 0)
        take_smaller(1, 1)
        for c in range(2):
            weigh_z(1, range(PACK), slice(c * P, (c + 1) * P))
            write_page(2 + c, round_z(2 + c), z2_mx)
